import numpy as np
import ml_dtypes


def mxq(x, axis, fmt="e4m3"):
    dtype, down = {"e4m3": (ml_dtypes.float8_e4m3fn, 7), "e5m2": (ml_dtypes.float8_e5m2, 14)}[fmt]
    v = np.moveaxis(np.asarray(x, np.float32).astype(ml_dtypes.bfloat16).astype(np.float64), axis, -1)
    blocks = v.reshape(v.shape[:-1] + (-1, 32))
    amax = np.abs(blocks).max(-1, keepdims=True)
    byte = np.maximum(np.where(amax > 0, np.frexp(amax)[1] - 1 + 127, 0) - down, 1)
    scale = np.exp2(byte - 127.0)
    codes = (blocks / scale).astype(np.float32).astype(dtype).astype(np.float64)
    return np.moveaxis((codes * scale).reshape(v.shape), -1, axis)


WIDE = False


def mx_kscale(k):
    if not WIDE:
        return np.ones(k)
    levels = np.array([10, -10, 5, -5, 0])
    if k % 512:
        return np.exp2(np.random.permutation(np.resize(levels, k // 32))).repeat(32)
    a = np.empty((k // 512, 16))
    for p in range(k // 512):
        a[p, :8] = np.random.permutation(np.resize(levels, 8))
        for g in range(8):
            far = levels[np.abs(levels - a[p, g]) >= 10]
            a[p, g + 8] = far[np.random.randint(len(far))]
    return np.exp2(a.ravel()).repeat(32)


def f64(x):
    return np.asarray(x).astype(np.float64)


def striped8(idx):
    return np.asarray(idx).reshape(8, -1, 16).transpose(0, 2, 1).reshape(128, -1).astype(np.uint16)


def unstriped8(offs):
    return offs.reshape(8, 16, -1).transpose(0, 2, 1).reshape(8, -1).astype(np.int64)


def pick8(x, idx, run):
    r = np.arange(len(x))
    return x[r[:, None], idx[r % (8 * run) // run]]


E2M1 = np.array([0.0, 0.5, 1.0, 1.5, 2.0, 3.0, 4.0, 6.0, -0.0, -0.5, -1.0, -1.5, -2.0, -3.0, -4.0, -6.0])


def pack_weight(w, fmt):
    k, n = w.shape
    w = f64(np.asarray(w, np.float32).astype(ml_dtypes.bfloat16)).reshape(k // 32, 32, n)
    amax = np.abs(w).max(1)
    if fmt == "e4m3":
        byte = np.frexp(amax)[1] - 1 + 127 - 7
    else:
        mant, ex = np.frexp(amax / 6.0)
        byte = np.where(mant > 0.5, ex, ex - 1) + 127
    byte = np.clip(np.where(amax > 0, byte, 1), 1, 254)
    scaled = (w * np.exp2(127.0 - byte)[:, None, :]).reshape(k, n).astype(np.float32)
    by_word = np.ascontiguousarray(scaled.reshape(k // 512, 128, 4, n).transpose(0, 1, 3, 2))
    if fmt == "e4m3":
        words = by_word.astype(ml_dtypes.float8_e4m3fn).view(np.uint8)
    else:
        c = by_word.astype(ml_dtypes.float4_e2m1fn).view(np.uint8) & 0xF
        words = (c[..., 0::2] | (c[..., 1::2] << 4)).reshape(k // 512, 128, 2 * n)
    return np.ascontiguousarray(words), np.ascontiguousarray(byte.astype(np.uint8).reshape(k // 512, 16, n))


def unpack_weight(words, scales, fmt):
    g, _, n = scales.shape
    words = np.ascontiguousarray(words).reshape(g, 128, n, -1)
    if fmt == "e4m3":
        vals = words.view(ml_dtypes.float8_e4m3fn).astype(np.float64)
    else:
        nib = np.empty((g, 128, n, 4), np.uint8)
        nib[..., 0::2] = words & 0xF
        nib[..., 1::2] = words >> 4
        vals = E2M1[nib]
    vals = vals * np.repeat(np.exp2(scales.astype(np.float64) - 127.0), 8, axis=1)[..., None]
    return vals.transpose(0, 1, 3, 2).reshape(g * 512, n)


D, T, I, Q = 512, 1024, 512, 128


def setup_inputs():
    n = np.random.standard_normal
    idx = np.stack([np.random.permutation(T)[:I] for _ in range(8)])
    idx2 = np.stack([np.random.permutation(T)[:I] for _ in range(8)])
    idx3 = np.stack([np.random.permutation(T)[:I] for _ in range(8)])
    idx4 = np.stack([np.random.permutation(T)[:I] for _ in range(8)])
    fd = mx_kscale(D)
    keysp = pack_weight(n((D, T)) / fd[:, None], "e4m3")
    return {
        "query": (n((D, Q)) * 0.9 / np.sqrt(D) * fd[:, None]).astype(np.float32),
        "keys_words": keysp[0],
        "keys_scales": keysp[1],
        "lam": (np.random.uniform(0.7, 1.3, (Q, 1))).astype(np.float32),
        "old": (np.random.uniform(0.3, 1.7, (Q, T))).astype(np.float32),
        "base": (0.5 * n((Q, T))).astype(np.float32),
        "offs": striped8(idx),
        "offs2": striped8(idx2),
        "offs3": striped8(idx3),
        "offs4": striped8(idx4),
    }


def reference(query, keys_words, keys_scales, lam, old, base, offs, offs2, offs3, offs4):
    idx = unstriped8(offs)
    idx2 = unstriped8(offs2)
    idx3 = unstriped8(offs3)
    idx4 = unstriped8(offs4)
    keysu = unpack_weight(keys_words, keys_scales, "e4m3")
    queryq = mxq(f64(query), 0, "e4m3")
    a = queryq.T @ keysu
    s = pick8(a, idx, 16) * f64(lam) - np.abs(pick8(a, idx2, 16) - pick8(a, idx3, 16))
    p = np.exp(s - np.max(s, axis=1, keepdims=True))
    w = p / np.sum(p, axis=1, keepdims=True)
    ws = w * pick8(f64(old), idx4, 16) * 256.0
    f1 = np.zeros((Q, T))
    f1[np.arange(Q)[:, None], idx[np.arange(Q) % 128 // 16]] = ws
    y = f64(base) + f1
    return y

@@ -1,0 +1,165 @@
+from contextlib import ExitStack
+
+import concourse.mybir as mybir
+
+D, T, SLOTS, Q = 512, 1024, 512, 128
+FLOPS = 2 * D * Q * T
+
+F32 = mybir.dt.float32
+BF16 = mybir.dt.bfloat16
+I32 = mybir.dt.int32
+U32 = mybir.dt.uint32
+U16 = mybir.dt.uint16
+U8 = mybir.dt.uint8
+FP8X4 = mybir.dt.float8_e4m3fn_x4
+ALU = mybir.AluOpType
+ACT = mybir.ActivationFunctionType
+
+P = 128
+PACK = 4
+LIST_COLS = SLOTS // 16
+HALF = SLOTS // 2
+KEY_LOADS = 2
+PASS_N = 256
+FIRST = 128
+OUT_CHUNK = 256
+
+
+def tile_attend_betweentwo_soft_timesold_heads_kernel(
+    tc, query, keys_words, keys_scales, lam, old, base, offs, offs2, offs3, offs4, out
+):
+    nc = tc.nc
+    with ExitStack() as ctx:
+        sb = ctx.enter_context(tc.tile_pool(name="sb", bufs=1))
+        psum = ctx.enter_context(tc.psum_pool(name="psum", bufs=1))
+
+        key_plane = sb.tile([P, T], U8, align_bytes=64)
+
+        q_raw = sb.tile([P, PACK, Q], F32)
+        nc.sync.dma_start(out=q_raw[:], in_=query.rearrange("(p j) q -> p j q", j=PACK))
+
+        words = keys_words[0].rearrange("p n t -> p (n t)")
+        load_cols = T // KEY_LOADS
+        key_codes = []
+        for c in range(KEY_LOADS):
+            codes = sb.tile([P, load_cols], U32, align_bytes=64, name=f"key_codes{c}")
+            nc.sync.dma_start(
+                out=codes[:].bitcast(I32),
+                in_=words[:, c * load_cols * PACK : (c + 1) * load_cols * PACK].bitcast(I32),
+            )
+            key_codes.append(codes)
+
+        for quad in range(4):
+            nc.scalar.dma_start(
+                out=key_plane[32 * quad : 32 * quad + 4, :].bitcast(I32),
+                in_=keys_scales[0, 4 * quad : 4 * quad + 4, :].bitcast(I32),
+            )
+
+        list3 = sb.tile([P, LIST_COLS], U16)
+        nc.sync.dma_start(list3[:], offs3)
+        list1 = sb.tile([P, LIST_COLS], U16)
+        nc.sync.dma_start(list1[:], offs)
+        list2 = sb.tile([P, LIST_COLS], U16)
+        nc.sync.dma_start(list2[:], offs2)
+        list4 = sb.tile([P, LIST_COLS], U16)
+        nc.sync.dma_start(list4[:], offs4)
+        lam_sb = sb.tile([P, 1], F32)
+        nc.sync.dma_start(out=lam_sb[:], in_=lam)
+        old_sb = sb.tile([P, T], F32)
+        nc.sync.dma_start(out=old_sb[:], in_=old)
+        base_sb = sb.tile([P, T], F32)
+        nc.sync.dma_start(out=base_sb[:], in_=base)
+
+        placed = sb.tile([P, T], F32)
+        nc.vector.memset(placed[:], 0.0)
+
+        q_bf = sb.tile([P, Q, PACK], BF16, align_bytes=64)
+        nc.vector.tensor_copy(out=q_bf[:], in_=q_raw[:].rearrange("p j q -> p q j"))
+        q_codes = sb.tile([P, Q], U32, align_bytes=64)
+        q_plane = sb.tile([P, Q], U8, align_bytes=64)
+        nc.vector.quantize_mx(
+            out=q_codes[:].bitcast(FP8X4), scales=q_plane[:], in_=q_bf[:].rearrange("p q j -> p (q j)")
+        )
+
+        a_sb = sb.tile([P, T], F32)
+        for n in range(T // PASS_N):
+            c, first = divmod(n * PASS_N, load_cols)
+            cols = slice(n * PASS_N, (n + 1) * PASS_N)
+            bank = psum.tile([P, PASS_N], F32, name=f"bank{n}")
+            nc.tensor.matmul_mx(
+                out=bank[:],
+                lhsT=q_codes[:].bitcast(FP8X4),
+                lhsT_scale=q_plane[:],
+                rhs=key_codes[c][:, first : first + PASS_N].bitcast(FP8X4),
+                rhs_scale=key_plane[:, cols],
+                start=True,
+                stop=True,
+            )
+            if n % 2 == 0:
+                nc.scalar.copy(out=a_sb[:, cols], in_=bank[:])
+            else:
+                nc.vector.tensor_copy(out=a_sb[:, cols], in_=bank[:])
+
+        def slots(h):
+            return slice(h * HALF, (h + 1) * HALF)
+
+        def entries(lst, first, count):
+            return lst[:, first // 16 : (first + count) // 16]
+
+        third = sb.tile([P, SLOTS], F32)
+        first0 = sb.tile([P, HALF], F32)
+        diff = sb.tile([P, SLOTS], F32)
+        dist = sb.tile([P, SLOTS], F32)
+        score = sb.tile([P, SLOTS], F32)
+
+        for h in range(2):
+            nc.scalar.activation(third[:, slots(h)], a_sb[:].indirect(entries(list3, h * HALF, HALF)), ACT.Copy)
+        nc.vector.tensor_copy(first0[:], a_sb[:].indirect(entries(list1, 0, HALF)))
+        for h in range(2):
+            nc.vector.tensor_tensor(
+                diff[:, slots(h)], a_sb[:].indirect(entries(list2, h * HALF, HALF)), third[:, slots(h)], ALU.subtract
+            )
+        first1 = third[:, slots(0)]
+        nc.vector.tensor_copy(first1, a_sb[:].indirect(entries(list1, HALF, HALF)))
+        for h in range(2):
+            nc.scalar.activation(dist[:, slots(h)], diff[:, slots(h)], ACT.Abs)
+        for h, first in enumerate((first0[:], first1)):
+            nc.vector.scalar_tensor_tensor(
+                out=score[:, slots(h)], in0=first, scalar=lam_sb[:], in1=dist[:, slots(h)],
+                op0=ALU.mult, op1=ALU.subtract,
+            )
+
+        old_picked = diff
+        nc.scalar.activation(old_picked[:], old_sb[:].indirect(list4[:]), ACT.Copy)
+
+        neg_max = sb.tile([P, 1], F32)
+        nc.vector.tensor_reduce(out=neg_max[:], in_=score[:], axis=mybir.AxisListType.X, op=ALU.max, negate=True)
+
+        prob = sb.tile([P, SLOTS], F32)
+        sums = sb.tile([P, 2], F32)
+        pieces = ((0, FIRST), (FIRST, SLOTS - FIRST))
+        for k, (first, count) in enumerate(pieces):
+            nc.scalar.activation(
+                prob[:, first : first + count], score[:, first : first + count], ACT.Exp,
+                bias=neg_max[:], accum_out=sums[:, k : k + 1],
+            )
+        for first, count in pieces:
+            nc.vector.tensor_tensor(
+                placed[:].indirect(entries(list1, first, count)),
+                prob[:, first : first + count], old_picked[:, first : first + count], ALU.mult,
+            )
+
+        sums_scaled = sb.tile([P, 2], F32)
+        total = sb.tile([P, 1], F32)
+        nc.scalar.activation(sums_scaled[:], sums[:], ACT.Copy, scale=1.0 / 256.0, accum_out=total[:])
+        factor = sb.tile([P, 1], F32)
+        nc.vector.reciprocal(factor[:], total[:])
+
+        result = sb.tile([P, T], F32)
+        for c in range(T // OUT_CHUNK):
+            cols = slice(c * OUT_CHUNK, (c + 1) * OUT_CHUNK)
+            nc.vector.scalar_tensor_tensor(
+                out=result[:, cols], in0=placed[:, cols], scalar=factor[:], in1=base_sb[:, cols],
+                op0=ALU.mult, op1=ALU.add,
+            )
+            nc.sync.dma_start(out=out[:, cols], in_=result[:, cols])

@@ -19,10 +19,11 @@ P = 128
 PACK = 4
 LIST_COLS = SLOTS // 16
 HALF = SLOTS // 2
-KEY_LOADS = 2
-PASS_N = 256
+KEY_LOADS = (256, 256, 512)
+PLANE_COLS = T // 4
+PASSES = (256, 256, 256, 128, 128)
 FIRST = 128
-OUT_CHUNK = 256
+OUT_CHUNKS = (256, 256, 256, 128, 128)
 
 
 def tile_attend_betweentwo_soft_timesold_heads_kernel(
@@ -33,27 +34,28 @@ def tile_attend_betweentwo_soft_timesold_heads_kernel(
         sb = ctx.enter_context(tc.tile_pool(name="sb", bufs=1))
         psum = ctx.enter_context(tc.psum_pool(name="psum", bufs=1))
 
-        key_plane = sb.tile([P, T], U8, align_bytes=64)
+        key_plane = sb.tile([P, PLANE_COLS], U8, align_bytes=64)
 
         q_raw = sb.tile([P, PACK, Q], F32)
         nc.sync.dma_start(out=q_raw[:], in_=query.rearrange("(p j) q -> p j q", j=PACK))
 
+        for quad in range(4):
+            nc.sync.dma_start(
+                out=key_plane[32 * quad : 32 * quad + 16, :].bitcast(I32),
+                in_=keys_scales[0, 4 * quad : 4 * quad + 4, :].bitcast(I32).rearrange("j (a c) -> a j c", a=4),
+            )
+
         words = keys_words[0].rearrange("p n t -> p (n t)")
-        load_cols = T // KEY_LOADS
         key_codes = []
-        for c in range(KEY_LOADS):
-            codes = sb.tile([P, load_cols], U32, align_bytes=64, name=f"key_codes{c}")
+        first = 0
+        for c, width in enumerate(KEY_LOADS):
+            codes = sb.tile([P, width], U32, align_bytes=64, name=f"key_codes{c}")
             nc.sync.dma_start(
                 out=codes[:].bitcast(I32),
-                in_=words[:, c * load_cols * PACK : (c + 1) * load_cols * PACK].bitcast(I32),
+                in_=words[:, first * PACK : (first + width) * PACK].bitcast(I32),
             )
-            key_codes.append(codes)
-
-        for quad in range(4):
-            nc.scalar.dma_start(
-                out=key_plane[32 * quad : 32 * quad + 4, :].bitcast(I32),
-                in_=keys_scales[0, 4 * quad : 4 * quad + 4, :].bitcast(I32),
-            )
+            key_codes.append((first, codes))
+            first = first + width
 
         list3 = sb.tile([P, LIST_COLS], U16)
         nc.sync.dma_start(list3[:], offs3)
@@ -74,58 +76,65 @@ def tile_attend_betweentwo_soft_timesold_heads_kernel(
         nc.vector.memset(placed[:], 0.0)
 
         q_bf = sb.tile([P, Q, PACK], BF16, align_bytes=64)
-        nc.vector.tensor_copy(out=q_bf[:], in_=q_raw[:].rearrange("p j q -> p q j"))
+        q_halves = (slice(0, Q // 2), slice(Q // 2, Q))
+        for rows in q_halves:
+            nc.vector.tensor_copy(
+                out=q_bf[:, rows, :].rearrange("p (c i) j -> p c j i", i=4),
+                in_=q_raw[:, :, rows].rearrange("p j (c i) -> p c j i", i=4),
+            )
         q_codes = sb.tile([P, Q], U32, align_bytes=64)
         q_plane = sb.tile([P, Q], U8, align_bytes=64)
-        nc.vector.quantize_mx(
-            out=q_codes[:].bitcast(FP8X4), scales=q_plane[:], in_=q_bf[:].rearrange("p q j -> p (q j)")
-        )
+        for rows in q_halves:
+            nc.vector.quantize_mx(
+                out=q_codes[:, rows].bitcast(FP8X4),
+                scales=q_plane[:, rows],
+                in_=q_bf[:, rows, :].rearrange("p q j -> p (q j)"),
+            )
 
         a_sb = sb.tile([P, T], F32)
-        for n in range(T // PASS_N):
-            c, first = divmod(n * PASS_N, load_cols)
-            cols = slice(n * PASS_N, (n + 1) * PASS_N)
-            bank = psum.tile([P, PASS_N], F32, name=f"bank{n}")
+        first = 0
+        for n, width in enumerate(PASSES):
+            load_first, codes = [load for load in key_codes if load[0] <= first][-1]
+            quarter, plane_first = divmod(first, PLANE_COLS)
+            bank = psum.tile([P, width], F32, name=f"bank{n}")
             nc.tensor.matmul_mx(
                 out=bank[:],
                 lhsT=q_codes[:].bitcast(FP8X4),
                 lhsT_scale=q_plane[:],
-                rhs=key_codes[c][:, first : first + PASS_N].bitcast(FP8X4),
-                rhs_scale=key_plane[:, cols],
+                rhs=codes[:, first - load_first : first - load_first + width].bitcast(FP8X4),
+                rhs_scale=key_plane[4 * quarter :, plane_first : plane_first + width],
                 start=True,
                 stop=True,
             )
-            if n % 2 == 0:
-                nc.scalar.copy(out=a_sb[:, cols], in_=bank[:])
-            else:
-                nc.vector.tensor_copy(out=a_sb[:, cols], in_=bank[:])
-
-        def slots(h):
-            return slice(h * HALF, (h + 1) * HALF)
+            copy = nc.vector.tensor_copy if n % 2 == 0 else nc.scalar.copy
+            copy(out=a_sb[:, first : first + width], in_=bank[:])
+            first = first + width
 
         def entries(lst, first, count):
             return lst[:, first // 16 : (first + count) // 16]
 
-        third = sb.tile([P, SLOTS], F32)
-        first0 = sb.tile([P, HALF], F32)
+        third_lo = sb.tile([P, HALF], F32)
+        third_hi = sb.tile([P, HALF], F32)
+        first_lo = sb.tile([P, HALF], F32)
         diff = sb.tile([P, SLOTS], F32)
         dist = sb.tile([P, SLOTS], F32)
         score = sb.tile([P, SLOTS], F32)
+        halves = (slice(0, HALF), slice(HALF, SLOTS))
 
-        for h in range(2):
-            nc.scalar.activation(third[:, slots(h)], a_sb[:].indirect(entries(list3, h * HALF, HALF)), ACT.Copy)
-        nc.vector.tensor_copy(first0[:], a_sb[:].indirect(entries(list1, 0, HALF)))
-        for h in range(2):
+        nc.scalar.activation(third_lo[:], a_sb[:].indirect(entries(list3, 0, HALF)), ACT.Copy)
+        nc.scalar.activation(third_hi[:], a_sb[:].indirect(entries(list3, HALF, HALF)), ACT.Copy)
+        nc.vector.tensor_copy(first_lo[:], a_sb[:].indirect(entries(list1, 0, HALF)))
+        for half, third in zip(halves, (third_lo, third_hi)):
             nc.vector.tensor_tensor(
-                diff[:, slots(h)], a_sb[:].indirect(entries(list2, h * HALF, HALF)), third[:, slots(h)], ALU.subtract
+                diff[:, half], a_sb[:].indirect(entries(list2, half.start, HALF)), third[:], ALU.subtract
             )
-        first1 = third[:, slots(0)]
-        nc.vector.tensor_copy(first1, a_sb[:].indirect(entries(list1, HALF, HALF)))
-        for h in range(2):
-            nc.scalar.activation(dist[:, slots(h)], diff[:, slots(h)], ACT.Abs)
-        for h, first in enumerate((first0[:], first1)):
+        first_hi = third_lo
+        nc.vector.tensor_copy(first_hi[:], a_sb[:].indirect(entries(list1, HALF, HALF)))
+        for half in halves:
+            nc.scalar.activation(dist[:, half], diff[:, half], ACT.Abs)
+        for half, picked in zip(halves, (first_lo, first_hi)):
             nc.vector.scalar_tensor_tensor(
-                out=score[:, slots(h)], in0=first, scalar=lam_sb[:], in1=dist[:, slots(h)],
+                out=score[:, half], in0=picked[:], scalar=lam_sb[:], in1=dist[:, half],
                 op0=ALU.mult, op1=ALU.subtract,
             )
 
@@ -156,8 +165,10 @@ def tile_attend_betweentwo_soft_timesold_heads_kernel(
         nc.vector.reciprocal(factor[:], total[:])
 
         result = sb.tile([P, T], F32)
-        for c in range(T // OUT_CHUNK):
-            cols = slice(c * OUT_CHUNK, (c + 1) * OUT_CHUNK)
+        first = 0
+        for width in OUT_CHUNKS:
+            cols = slice(first, first + width)
+            first = first + width
             nc.vector.scalar_tensor_tensor(
                 out=result[:, cols], in0=placed[:, cols], scalar=factor[:], in1=base_sb[:, cols],
                 op0=ALU.mult, op1=ALU.add,

@@ -59,10 +59,10 @@ def tile_attend_betweentwo_soft_timesold_heads_kernel(
 
         list3 = sb.tile([P, LIST_COLS], U16)
         nc.sync.dma_start(list3[:], offs3)
-        list1 = sb.tile([P, LIST_COLS], U16)
-        nc.sync.dma_start(list1[:], offs)
         list2 = sb.tile([P, LIST_COLS], U16)
         nc.sync.dma_start(list2[:], offs2)
+        list1 = sb.tile([P, LIST_COLS], U16)
+        nc.sync.dma_start(list1[:], offs)
         list4 = sb.tile([P, LIST_COLS], U16)
         nc.sync.dma_start(list4[:], offs4)
         lam_sb = sb.tile([P, 1], F32)
@@ -114,31 +114,32 @@ def tile_attend_betweentwo_soft_timesold_heads_kernel(
             return lst[:, first // 16 : (first + count) // 16]
 
         third_lo = sb.tile([P, HALF], F32)
-        third_hi = sb.tile([P, HALF], F32)
-        first_lo = sb.tile([P, HALF], F32)
+        pair_hi = sb.tile([P, SLOTS], F32)
+        picked = sb.tile([P, SLOTS], F32)
         diff = sb.tile([P, SLOTS], F32)
         dist = sb.tile([P, SLOTS], F32)
         score = sb.tile([P, SLOTS], F32)
-        halves = (slice(0, HALF), slice(HALF, SLOTS))
+        lo, hi = slice(0, HALF), slice(HALF, SLOTS)
+        third_hi, second_hi = pair_hi[:, lo], pair_hi[:, hi]
 
-        nc.scalar.activation(third_lo[:], a_sb[:].indirect(entries(list3, 0, HALF)), ACT.Copy)
-        nc.scalar.activation(third_hi[:], a_sb[:].indirect(entries(list3, HALF, HALF)), ACT.Copy)
-        nc.vector.tensor_copy(first_lo[:], a_sb[:].indirect(entries(list1, 0, HALF)))
-        for half, third in zip(halves, (third_lo, third_hi)):
-            nc.vector.tensor_tensor(
-                diff[:, half], a_sb[:].indirect(entries(list2, half.start, HALF)), third[:], ALU.subtract
-            )
-        first_hi = third_lo
-        nc.vector.tensor_copy(first_hi[:], a_sb[:].indirect(entries(list1, HALF, HALF)))
-        for half in halves:
-            nc.scalar.activation(dist[:, half], diff[:, half], ACT.Abs)
-        for half, picked in zip(halves, (first_lo, first_hi)):
+        nc.vector.tensor_copy(third_lo[:], a_sb[:].indirect(entries(list3, 0, HALF)))
+        nc.scalar.activation(third_hi, a_sb[:].indirect(entries(list3, HALF, HALF)), ACT.Copy)
+        nc.scalar.activation(second_hi, a_sb[:].indirect(entries(list2, HALF, HALF)), ACT.Copy)
+        for half in (lo, hi):
+            nc.scalar.activation(picked[:, half], a_sb[:].indirect(entries(list1, half.start, HALF)), ACT.Copy)
+        nc.vector.tensor_tensor(diff[:, lo], a_sb[:].indirect(entries(list2, 0, HALF)), third_lo[:], ALU.subtract)
+        nc.vector.tensor_tensor(diff[:, hi], second_hi, third_hi, ALU.subtract)
+        for half in (lo, hi):
             nc.vector.scalar_tensor_tensor(
-                out=score[:, half], in0=picked[:], scalar=lam_sb[:], in1=dist[:, half],
+                out=dist[:, half], in0=diff[:, half], scalar=-1.0, in1=diff[:, half], op0=ALU.mult, op1=ALU.max
+            )
+        for half in (lo, hi):
+            nc.vector.scalar_tensor_tensor(
+                out=score[:, half], in0=picked[:, half], scalar=lam_sb[:], in1=dist[:, half],
                 op0=ALU.mult, op1=ALU.subtract,
             )
 
-        old_picked = diff
+        old_picked = pair_hi
         nc.scalar.activation(old_picked[:], old_sb[:].indirect(list4[:]), ACT.Copy)
 
         neg_max = sb.tile([P, 1], F32)

from contextlib import ExitStack

import concourse.mybir as mybir

D, T, SLOTS, Q = 512, 1024, 512, 128
FLOPS = 2 * D * Q * T

F32 = mybir.dt.float32
BF16 = mybir.dt.bfloat16
I32 = mybir.dt.int32
U32 = mybir.dt.uint32
U16 = mybir.dt.uint16
U8 = mybir.dt.uint8
FP8X4 = mybir.dt.float8_e4m3fn_x4
ALU = mybir.AluOpType
ACT = mybir.ActivationFunctionType

P = 128
PACK = 4
LIST_COLS = SLOTS // 16
HALF = SLOTS // 2
KEY_LOADS = (256, 256, 512)
PLANE_COLS = T // 4
PASSES = (256, 256, 256, 128, 128)
FIRST = 128
OUT_CHUNKS = (256, 256, 256, 128, 128)


def tile_attend_betweentwo_soft_timesold_heads_kernel(
    tc, query, keys_words, keys_scales, lam, old, base, offs, offs2, offs3, offs4, out
):
    nc = tc.nc
    with ExitStack() as ctx:
        sb = ctx.enter_context(tc.tile_pool(name="sb", bufs=1))
        psum = ctx.enter_context(tc.psum_pool(name="psum", bufs=1))

        key_plane = sb.tile([P, PLANE_COLS], U8, align_bytes=64)

        q_raw = sb.tile([P, PACK, Q], F32)
        nc.sync.dma_start(out=q_raw[:], in_=query.rearrange("(p j) q -> p j q", j=PACK))

        for quad in range(4):
            nc.sync.dma_start(
                out=key_plane[32 * quad : 32 * quad + 16, :].bitcast(I32),
                in_=keys_scales[0, 4 * quad : 4 * quad + 4, :].bitcast(I32).rearrange("j (a c) -> a j c", a=4),
            )

        words = keys_words[0].rearrange("p n t -> p (n t)")
        key_codes = []
        first = 0
        for c, width in enumerate(KEY_LOADS):
            codes = sb.tile([P, width], U32, align_bytes=64, name=f"key_codes{c}")
            nc.sync.dma_start(
                out=codes[:].bitcast(I32),
                in_=words[:, first * PACK : (first + width) * PACK].bitcast(I32),
            )
            key_codes.append((first, codes))
            first = first + width

        list3 = sb.tile([P, LIST_COLS], U16)
        nc.sync.dma_start(list3[:], offs3)
        list2 = sb.tile([P, LIST_COLS], U16)
        nc.sync.dma_start(list2[:], offs2)
        list1 = sb.tile([P, LIST_COLS], U16)
        nc.sync.dma_start(list1[:], offs)
        list4 = sb.tile([P, LIST_COLS], U16)
        nc.sync.dma_start(list4[:], offs4)
        lam_sb = sb.tile([P, 1], F32)
        nc.sync.dma_start(out=lam_sb[:], in_=lam)
        old_sb = sb.tile([P, T], F32)
        nc.sync.dma_start(out=old_sb[:], in_=old)
        base_sb = sb.tile([P, T], F32)
        nc.sync.dma_start(out=base_sb[:], in_=base)

        placed = sb.tile([P, T], F32)
        nc.vector.memset(placed[:], 0.0)

        q_bf = sb.tile([P, Q, PACK], BF16, align_bytes=64)
        q_halves = (slice(0, Q // 2), slice(Q // 2, Q))
        for rows in q_halves:
            nc.vector.tensor_copy(
                out=q_bf[:, rows, :].rearrange("p (c i) j -> p c j i", i=4),
                in_=q_raw[:, :, rows].rearrange("p j (c i) -> p c j i", i=4),
            )
        q_codes = sb.tile([P, Q], U32, align_bytes=64)
        q_plane = sb.tile([P, Q], U8, align_bytes=64)
        for rows in q_halves:
            nc.vector.quantize_mx(
                out=q_codes[:, rows].bitcast(FP8X4),
                scales=q_plane[:, rows],
                in_=q_bf[:, rows, :].rearrange("p q j -> p (q j)"),
            )

        a_sb = sb.tile([P, T], F32)
        first = 0
        for n, width in enumerate(PASSES):
            load_first, codes = [load for load in key_codes if load[0] <= first][-1]
            quarter, plane_first = divmod(first, PLANE_COLS)
            bank = psum.tile([P, width], F32, name=f"bank{n}")
            nc.tensor.matmul_mx(
                out=bank[:],
                lhsT=q_codes[:].bitcast(FP8X4),
                lhsT_scale=q_plane[:],
                rhs=codes[:, first - load_first : first - load_first + width].bitcast(FP8X4),
                rhs_scale=key_plane[4 * quarter :, plane_first : plane_first + width],
                start=True,
                stop=True,
            )
            copy = nc.vector.tensor_copy if n % 2 == 0 else nc.scalar.copy
            copy(out=a_sb[:, first : first + width], in_=bank[:])
            first = first + width

        def entries(lst, first, count):
            return lst[:, first // 16 : (first + count) // 16]

        third_lo = sb.tile([P, HALF], F32)
        pair_hi = sb.tile([P, SLOTS], F32)
        picked = sb.tile([P, SLOTS], F32)
        diff = sb.tile([P, SLOTS], F32)
        dist = sb.tile([P, SLOTS], F32)
        score = sb.tile([P, SLOTS], F32)
        lo, hi = slice(0, HALF), slice(HALF, SLOTS)
        third_hi, second_hi = pair_hi[:, lo], pair_hi[:, hi]

        nc.vector.tensor_copy(third_lo[:], a_sb[:].indirect(entries(list3, 0, HALF)))
        nc.scalar.activation(third_hi, a_sb[:].indirect(entries(list3, HALF, HALF)), ACT.Copy)
        nc.scalar.activation(second_hi, a_sb[:].indirect(entries(list2, HALF, HALF)), ACT.Copy)
        for half in (lo, hi):
            nc.scalar.activation(picked[:, half], a_sb[:].indirect(entries(list1, half.start, HALF)), ACT.Copy)
        nc.vector.tensor_tensor(diff[:, lo], a_sb[:].indirect(entries(list2, 0, HALF)), third_lo[:], ALU.subtract)
        nc.vector.tensor_tensor(diff[:, hi], second_hi, third_hi, ALU.subtract)
        for half in (lo, hi):
            nc.vector.scalar_tensor_tensor(
                out=dist[:, half], in0=diff[:, half], scalar=-1.0, in1=diff[:, half], op0=ALU.mult, op1=ALU.max
            )
        for half in (lo, hi):
            nc.vector.scalar_tensor_tensor(
                out=score[:, half], in0=picked[:, half], scalar=lam_sb[:], in1=dist[:, half],
                op0=ALU.mult, op1=ALU.subtract,
            )

        old_picked = pair_hi
        nc.scalar.activation(old_picked[:], old_sb[:].indirect(list4[:]), ACT.Copy)

        neg_max = sb.tile([P, 1], F32)
        nc.vector.tensor_reduce(out=neg_max[:], in_=score[:], axis=mybir.AxisListType.X, op=ALU.max, negate=True)

        prob = sb.tile([P, SLOTS], F32)
        sums = sb.tile([P, 2], F32)
        pieces = ((0, FIRST), (FIRST, SLOTS - FIRST))
        for k, (first, count) in enumerate(pieces):
            nc.scalar.activation(
                prob[:, first : first + count], score[:, first : first + count], ACT.Exp,
                bias=neg_max[:], accum_out=sums[:, k : k + 1],
            )
        for first, count in pieces:
            nc.vector.tensor_tensor(
                placed[:].indirect(entries(list1, first, count)),
                prob[:, first : first + count], old_picked[:, first : first + count], ALU.mult,
            )

        sums_scaled = sb.tile([P, 2], F32)
        total = sb.tile([P, 1], F32)
        nc.scalar.activation(sums_scaled[:], sums[:], ACT.Copy, scale=1.0 / 256.0, accum_out=total[:])
        factor = sb.tile([P, 1], F32)
        nc.vector.reciprocal(factor[:], total[:])

        result = sb.tile([P, T], F32)
        first = 0
        for width in OUT_CHUNKS:
            cols = slice(first, first + width)
            first = first + width
            nc.vector.scalar_tensor_tensor(
                out=result[:, cols], in0=placed[:, cols], scalar=factor[:], in1=base_sb[:, cols],
                op0=ALU.mult, op1=ALU.add,
            )
            nc.sync.dma_start(out=out[:, cols], in_=result[:, cols])
